import numpy as np
import ml_dtypes


def mxq(x, axis, fmt="e4m3"):
    dtype, down = {"e4m3": (ml_dtypes.float8_e4m3fn, 7), "e5m2": (ml_dtypes.float8_e5m2, 14)}[fmt]
    v = np.moveaxis(np.asarray(x, np.float32).astype(ml_dtypes.bfloat16).astype(np.float64), axis, -1)
    blocks = v.reshape(v.shape[:-1] + (-1, 32))
    amax = np.abs(blocks).max(-1, keepdims=True)
    byte = np.maximum(np.where(amax > 0, np.frexp(amax)[1] - 1 + 127, 0) - down, 1)
    scale = np.exp2(byte - 127.0)
    codes = (blocks / scale).astype(np.float32).astype(dtype).astype(np.float64)
    return np.moveaxis((codes * scale).reshape(v.shape), -1, axis)


WIDE = False


def mx_kscale(k):
    if not WIDE:
        return np.ones(k)
    levels = np.array([10, -10, 5, -5, 0])
    if k % 512:
        return np.exp2(np.random.permutation(np.resize(levels, k // 32))).repeat(32)
    a = np.empty((k // 512, 16))
    for p in range(k // 512):
        a[p, :8] = np.random.permutation(np.resize(levels, 8))
        for g in range(8):
            far = levels[np.abs(levels - a[p, g]) >= 10]
            a[p, g + 8] = far[np.random.randint(len(far))]
    return np.exp2(a.ravel()).repeat(32)


def f64(x):
    return np.asarray(x).astype(np.float64)


def striped(idx):
    return np.tile(idx.reshape(-1, 16).T, (8, 1)).astype(np.uint16)


def unstriped(offs):
    return offs[:16].T.reshape(-1).astype(np.int64)


def pack_weight(w):
    k, n = w.shape
    w = f64(np.asarray(w, np.float32).astype(ml_dtypes.bfloat16)).reshape(k // 32, 32, n)
    amax = np.abs(w).max(1)
    byte = np.clip(np.where(amax > 0, np.frexp(amax)[1] - 1 + 127 - 7, 1), 1, 254)
    scaled = (w * np.exp2(127.0 - byte)[:, None, :]).reshape(k, n).astype(np.float32)
    words = np.ascontiguousarray(scaled.reshape(k // 512, 128, 4, n).transpose(0, 1, 3, 2)).astype(ml_dtypes.float8_e4m3fn).view(np.uint8)
    return words, np.ascontiguousarray(byte.astype(np.uint8).reshape(k // 512, 16, n))


def unpack_weight(words, scales):
    g, p, n, _ = words.shape
    vals = np.ascontiguousarray(words).view(ml_dtypes.float8_e4m3fn).astype(np.float64) * np.repeat(np.exp2(scales.astype(np.float64) - 127.0), 8, axis=1)[..., None]
    return vals.transpose(0, 1, 3, 2).reshape(g * 512, n)


E2M1 = np.array([0.0, 0.5, 1.0, 1.5, 2.0, 3.0, 4.0, 6.0, -0.0, -0.5, -1.0, -1.5, -2.0, -3.0, -4.0, -6.0])


def pack_fp4(w):
    k, n = w.shape
    w = f64(np.asarray(w, np.float32).astype(ml_dtypes.bfloat16)).reshape(k // 32, 32, n)
    amax = np.abs(w).max(1)
    mant, ex = np.frexp(amax / 6.0)
    byte = np.clip(np.where(amax > 0, np.where(mant > 0.5, ex, ex - 1) + 127, 1), 1, 254)
    scaled = (w * np.exp2(127.0 - byte)[:, None, :]).reshape(k, n).astype(np.float32)
    c = np.ascontiguousarray(scaled.reshape(k // 512, 128, 4, n).transpose(0, 1, 3, 2)).astype(ml_dtypes.float4_e2m1fn).view(np.uint8) & 0xF
    words = (c[..., 0::2] | (c[..., 1::2] << 4)).reshape(k // 512, 128, 2 * n)
    return np.ascontiguousarray(words), np.ascontiguousarray(byte.astype(np.uint8).reshape(k // 512, 16, n))


def unpack_fp4(words, scales):
    g, _, n = scales.shape
    words = np.ascontiguousarray(words).reshape(g, 128, n, 2)
    nib = np.empty((g, 128, n, 4), np.uint8)
    nib[..., 0::2] = words & 0xF
    nib[..., 1::2] = words >> 4
    vals = E2M1[nib] * np.repeat(np.exp2(scales.astype(np.float64) - 127.0), 8, axis=1)[..., None]
    return vals.transpose(0, 1, 3, 2).reshape(g * 512, n)


K, T, S, D, H, Z, W = 512, 2048, 512, 2, 512, 512, 2048
P = 2 ** 7


def setup_inputs():
    n = np.random.standard_normal
    s = mx_kscale(K)[:, None]
    u = mx_kscale(H)
    packed_xT = pack_weight(n((K, T)) * s)
    packed_w1 = pack_fp4(n((K, H)) / np.sqrt(K) / s)
    packed_eT = pack_weight(n((K, W)) * s)
    packed_w2 = pack_fp4(n((K, H)) / np.sqrt(K) / s)
    return {
        "x_words": packed_xT[0],
        "x_scales": packed_xT[1],
        "w1_words": packed_w1[0],
        "w1_scales": packed_w1[1],
        "e_words": packed_eT[0],
        "e_scales": packed_eT[1],
        "w2_words": packed_w2[0],
        "w2_scales": packed_w2[1],
        "unit": (np.random.uniform(0.6, 1.4, (H, 1)) * u[:, None]).astype(np.float32),
        "unit2": (np.random.uniform(0.6, 1.4, (H, 1)) / np.sqrt(H) / u[:, None]).astype(np.float32),
        "fert": (np.tile(np.random.uniform(0.4, 1.6, W), (P, 1))).astype(np.float32),
        "offs": striped(np.random.permutation(T)[:S]),
        "tgt": striped(np.random.permutation(W)[:Z]),
        "mor": striped(np.random.permutation(Z)),
        "dia": striped(np.random.permutation(Z)),
    }


def reference(x_words, x_scales, w1_words, w1_scales, e_words, e_scales, w2_words, w2_scales, unit, unit2, fert, offs, tgt, mor, dia):
    xq = unpack_weight(x_words, x_scales)[:, unstriped(offs)]
    y = unpack_fp4(w1_words, w1_scales).T @ xq
    word = y.reshape(len(y), -1, D).max(axis=2) + 0.5 * (y.reshape(len(y), -1, D).min(axis=2))
    hid = f64(unit) * word
    e_tgt = unpack_weight(e_words, e_scales)[:, unstriped(tgt)]
    ye = unpack_fp4(w2_words, w2_scales).T @ e_tgt
    em_ = ye[:, unstriped(mor)]
    tw = np.maximum(ye, 0.7 * em_)
    hid2 = f64(unit2) * tw
    sc = mxq(hid, 0, "e4m3").T @ mxq(hid2, 0, "e4m3")
    top = sc.max(axis=1, keepdims=True)
    ew = np.exp(sc - top)
    tot = ew.sum(axis=1, keepdims=True)
    pr = 50.0 * (ew / tot)
    return np.sqrt(pr * pr[:, unstriped(dia)] + 0.01) + (0.2 * sc) * (f64(fert)[:1][:, unstriped(tgt)])

@@ -1,0 +1,240 @@
+from contextlib import ExitStack
+
+import concourse.mybir as mybir
+
+K, T, S, H, V = 512, 2048, 512, 512, 256
+FLOPS = 2 * K * H * S * 2 + 2 * H * V * S
+
+F32 = mybir.dt.float32
+BF16 = mybir.dt.bfloat16
+I32 = mybir.dt.int32
+U32 = mybir.dt.uint32
+U16 = mybir.dt.uint16
+U8 = mybir.dt.uint8
+FP8X4 = mybir.dt.float8_e4m3fn_x4
+FP4X4 = mybir.dt.float4_e2m1fn_x4
+ALU = mybir.AluOpType
+ACT = mybir.ActivationFunctionType
+AX = mybir.AxisListType
+
+P = 128
+PACK = 4
+HALF = S // 2
+
+
+def tile_picked_ywordal_geo_p_kernel(
+    tc, x_words, x_scales, w1_words, w1_scales, e_words, e_scales, w2_words, w2_scales,
+    unit, unit2, fert, offs, tgt, mor, dia, out,
+):
+    nc = tc.nc
+    with ExitStack() as ctx:
+        sb = ctx.enter_context(tc.tile_pool(name="sb", bufs=1))
+        ps = ctx.enter_context(tc.psum_pool(name="ps", bufs=1))
+
+        def new(shape, dtype, name):
+            return sb.tile(shape, dtype, name=name, align_bytes=64)
+
+        def load_list(src, name):
+            t = sb.tile([P, S // 16], U16, name=name)
+            nc.sync.dma_start(t[:], src)
+            return t
+
+        def load_scales(plane, src):
+            for q in range(4):
+                nc.sync.dma_start(
+                    plane[32 * q : 32 * q + 4, :].bitcast(I32),
+                    src[0, 4 * q : 4 * q + 4, :].bitcast(I32),
+                )
+
+        def load_table(src, name):
+            t = new([P, T], I32, name)
+            nc.sync.dma_start(t[:], src[0].rearrange("p n r -> p (n r)").bitcast(I32))
+            return t
+
+        def load_weight_words(src, name):
+            t = new([P, 2 * H], U8, name)
+            nc.sync.dma_start(t[:].bitcast(I32), src[0].bitcast(I32))
+            return t
+
+        def load_factor(src, name):
+            t = new([P, PACK], F32, name)
+            nc.sync.dma_start(t[:], src.rearrange("(p t) o -> p (t o)", t=PACK))
+            return t
+
+        e_plane = new([P, T], U8, "e_plane")
+        x_plane = new([P, T], U8, "x_plane")
+        w2_plane = new([P, H], U8, "w2_plane")
+        w1_plane = new([P, H], U8, "w1_plane")
+        for plane in (e_plane, w2_plane, x_plane, w1_plane):
+            nc.vector.memset(plane[:].bitcast(I32), 0)
+
+        tgt_sb = load_list(tgt, "tgt_sb")
+        load_scales(e_plane, e_scales)
+        e_table = load_table(e_words, "e_table")
+        w2_raw = load_weight_words(w2_words, "w2_raw")
+        load_scales(w2_plane, w2_scales)
+        unit2_sb = load_factor(unit2, "unit2_sb")
+        x_table = load_table(x_words, "x_table")
+        offs_sb = load_list(offs, "offs_sb")
+        load_scales(x_plane, x_scales)
+        mor_sb = load_list(mor, "mor_sb")
+        w1_raw = load_weight_words(w1_words, "w1_raw")
+        load_scales(w1_plane, w1_scales)
+        unit_sb = load_factor(unit, "unit_sb")
+        dia_sb = load_list(dia, "dia_sb")
+        fert_sb = new([P, T], F32, "fert_sb")
+        nc.sync.dma_start(fert_sb[:], fert)
+
+        def deal(raw, plane, name):
+            words = new([P, 2 * H], U8, name + "_words")
+            scales = new([P, H], U8, name + "_scales")
+            nc.scalar.copy(
+                words[:].bitcast(U16).rearrange("p (t m) -> p t m", t=PACK),
+                raw[:].bitcast(U16).rearrange("p (m t) -> p t m", t=PACK),
+            )
+            nc.gpsimd.tensor_copy(
+                scales[:].rearrange("p (t m) -> p t m", t=PACK),
+                plane[:].rearrange("p (m t) -> p t m", t=PACK),
+            )
+            return words, scales
+
+        def pick(table, plane, lst, name):
+            scales = new([P, S], U8, name + "_scales")
+            words = new([P, S], U32, name + "_words")
+            nc.vector.tensor_copy(scales[:], plane[:].indirect(lst[:]))
+            nc.vector.tensor_copy(words[:], table[:].bitcast(U32).indirect(lst[:]))
+            return words, scales
+
+        def first_product(w, picked, tag):
+            banks = []
+            for t in range(PACK):
+                bank = ps.tile([P, S], F32, name="%s%d" % (tag, t))
+                nc.tensor.matmul_mx(
+                    out=bank[:],
+                    lhsT=w[0][:, 2 * P * t : 2 * P * (t + 1)].bitcast(FP4X4),
+                    lhsT_scale=w[1][:, P * t : P * (t + 1)],
+                    rhs=picked[0][:].bitcast(FP8X4),
+                    rhs_scale=picked[1][:],
+                    start=True, stop=True,
+                )
+                banks.append(bank)
+            return banks
+
+        size2 = new([P, PACK], F32, "size2")
+        sign2 = new([P, PACK], F32, "sign2")
+        nc.scalar.activation(size2[:], unit2_sb[:], ACT.Abs)
+        nc.scalar.activation(sign2[:], unit2_sb[:], ACT.Sign)
+        w2 = deal(w2_raw, w2_plane, "w2")
+        e_pick = pick(e_table, e_plane, tgt_sb, "e_pick")
+        ye = first_product(w2, e_pick, "ye")
+        ye_sb = new([P, PACK, S], F32, "ye_sb")
+        for t in range(PACK):
+            nc.scalar.activation(ye_sb[:, t, :], ye[t][:], ACT.Copy, scale=size2[:, t : t + 1])
+
+        x_pick = pick(x_table, x_plane, offs_sb, "x_pick")
+        w1 = deal(w1_raw, w1_plane, "w1")
+        y = first_product(w1, x_pick, "y")
+        fac = new([P, PACK], F32, "fac")
+        pos = new([P, PACK], F32, "pos")
+        beta = new([P, PACK], F32, "beta")
+        rho = new([P, PACK], F32, "rho")
+        fac_lo = new([P, PACK], F32, "fac_lo")
+        nc.gpsimd.tensor_tensor(fac[:], unit_sb[:], sign2[:], ALU.mult)
+        nc.gpsimd.tensor_scalar(pos[:], fac[:], 0.0, None, ALU.is_ge)
+        nc.gpsimd.tensor_scalar(beta[:], pos[:], -0.5, 1.0, ALU.mult, ALU.add)
+        nc.gpsimd.tensor_scalar(rho[:], pos[:], 1.5, 0.5, ALU.mult, ALU.add)
+        nc.gpsimd.tensor_tensor(fac_lo[:], fac[:], beta[:], ALU.mult)
+
+        first = new([P, PACK, V], F32, "first")
+        big = new([P, PACK, V], F32, "big")
+        small = new([P, PACK, V], F32, "small")
+        hid_rows = new([P, PACK, V], BF16, "hid_rows")
+        for t in range(PACK):
+            pair = y[t][:].rearrange("p (v d) -> p v d", d=2)
+            col = fac_lo[:, t : t + 1]
+            nc.scalar.activation(first[:, t, :], pair[:, :, 0], ACT.Copy, scale=col)
+            nc.vector.scalar_tensor_tensor(big[:, t, :], pair[:, :, 1], col, first[:, t, :], ALU.mult, ALU.max)
+            nc.vector.scalar_tensor_tensor(small[:, t, :], pair[:, :, 1], col, first[:, t, :], ALU.mult, ALU.min)
+        for t in range(PACK):
+            nc.vector.scalar_tensor_tensor(
+                hid_rows[:, t, :], big[:, t, :], rho[:, t : t + 1], small[:, t, :], ALU.mult, ALU.add)
+        hid = new([P, V, PACK], BF16, "hid")
+        nc.vector.tensor_copy(
+            hid[:].rearrange("p (c i) t -> p c t i", i=4),
+            hid_rows[:].rearrange("p t (c i) -> p c t i", i=4),
+        )
+        hid_codes = new([P, V], U32, "hid_codes")
+        hid_scales = new([P, V], U8, "hid_scales")
+
+        related = new([P, PACK, S], F32, "related")
+        hid2 = new([P, S, PACK], BF16, "hid2")
+        hid2_codes = new([P, S], U32, "hid2_codes")
+        hid2_scales = new([P, S], U8, "hid2_scales")
+        for h in range(2):
+            cols = slice(HALF * h, HALF * (h + 1))
+            for t in range(PACK):
+                nc.scalar.activation(
+                    related[:, t, cols],
+                    ye_sb[:, t, :].indirect(mor_sb[:, 16 * h : 16 * (h + 1)]),
+                    ACT.Copy, scale=0.7,
+                )
+            nc.vector.tensor_tensor(
+                hid2[:, cols, :].rearrange("p (c i) t -> p c t i", i=4),
+                related[:, :, cols].rearrange("p t (c i) -> p c t i", i=4),
+                ye_sb[:, :, cols].rearrange("p t (c i) -> p c t i", i=4),
+                ALU.max,
+            )
+            if h == 0:
+                nc.vector.quantize_mx(
+                    out=hid_codes[:].bitcast(FP8X4), scales=hid_scales[:],
+                    in_=hid[:].rearrange("p v t -> p (v t)"),
+                )
+            nc.vector.quantize_mx(
+                out=hid2_codes[:, cols].bitcast(FP8X4), scales=hid2_scales[:, cols],
+                in_=hid2[:, cols, :].rearrange("p e t -> p (e t)"),
+            )
+
+        fert_pick = new([P, S], F32, "fert_pick")
+        nc.scalar.activation(fert_pick[:], fert_sb[:].indirect(tgt_sb[:]), ACT.Copy, scale=0.2)
+
+        sc = [ps.tile([P, S], F32, name="ye%d" % m) for m in range(2)]
+        for h in range(2):
+            cols = slice(HALF * h, HALF * (h + 1))
+            for m in range(2):
+                rows = slice(P * m, P * (m + 1))
+                nc.tensor.matmul_mx(
+                    out=sc[m][:, cols],
+                    lhsT=hid_codes[:, rows].bitcast(FP8X4), lhsT_scale=hid_scales[:, rows],
+                    rhs=hid2_codes[:, cols].bitcast(FP8X4), rhs_scale=hid2_scales[:, cols],
+                    start=True, stop=True,
+                )
+
+        neg_top = [new([P, 1], F32, "neg_top%d" % m) for m in range(2)]
+        tot = new([P, 2], F32, "tot")
+        ew = [new([P, S], F32, "ew%d" % m) for m in range(2)]
+        ew_copy = [new([P, S], F32, "ew_copy%d" % m) for m in range(2)]
+        prod = [new([P, S], F32, "prod%d" % m) for m in range(2)]
+        side = [new([P, S], F32, "side%d" % m) for m in range(2)]
+        root = [new([P, S], F32, "root%d" % m) for m in range(2)]
+        res = [new([P, S], F32, "res%d" % m) for m in range(2)]
+        for m in range(2):
+            nc.vector.tensor_reduce(neg_top[m][:], sc[m][:], AX.X, ALU.max, negate=True)
+            nc.scalar.activation(ew[m][:], sc[m][:], ACT.Exp, bias=neg_top[m][:], accum_out=tot[:, m : m + 1])
+        inv = new([P, 2], F32, "inv")
+        gain = new([P, 2], F32, "gain")
+        for m in range(2):
+            nc.vector.tensor_copy(ew_copy[m][:], ew[m][:])
+            for h in range(2):
+                cols = slice(HALF * h, HALF * (h + 1))
+                nc.vector.tensor_tensor(
+                    prod[m][:, cols], ew[m][:].indirect(dia_sb[:, 16 * h : 16 * (h + 1)]),
+                    ew_copy[m][:, cols], ALU.mult,
+                )
+            if m == 0:
+                nc.vector.reciprocal(inv[:], tot[:])
+                nc.vector.scalar_tensor_tensor(gain[:], inv[:], 2500.0, inv[:], ALU.mult, ALU.mult)
+        for m in range(2):
+            nc.vector.tensor_tensor(side[m][:], sc[m][:], fert_pick[:], ALU.mult)
+            nc.scalar.activation(root[m][:], prod[m][:], ACT.Sqrt, bias=0.01, scale=gain[:, m : m + 1])
+            nc.vector.tensor_tensor(res[m][:], root[m][:], side[m][:], ALU.add)
+            nc.sync.dma_start(out[P * m : P * (m + 1), :], res[m][:])

@@ -20,6 +20,7 @@ AX = mybir.AxisListType
 P = 128
 PACK = 4
 HALF = S // 2
+PIECES = ((0, 128), (128, 384), (384, 512))
 
 
 def tile_picked_ywordal_geo_p_kernel(
@@ -39,9 +40,9 @@ def tile_picked_ywordal_geo_p_kernel(
             nc.sync.dma_start(t[:], src)
             return t
 
-        def load_scales(plane, src):
+        def load_scales(plane, src, queue):
             for q in range(4):
-                nc.sync.dma_start(
+                queue.dma_start(
                     plane[32 * q : 32 * q + 4, :].bitcast(I32),
                     src[0, 4 * q : 4 * q + 4, :].bitcast(I32),
                 )
@@ -51,36 +52,39 @@ def tile_picked_ywordal_geo_p_kernel(
             nc.sync.dma_start(t[:], src[0].rearrange("p n r -> p (n r)").bitcast(I32))
             return t
 
-        def load_weight_words(src, name):
+        def load_weight_words(src, name, queue):
             t = new([P, 2 * H], U8, name)
-            nc.sync.dma_start(t[:].bitcast(I32), src[0].bitcast(I32))
+            queue.dma_start(t[:].bitcast(I32), src[0].bitcast(I32))
             return t
 
-        def load_factor(src, name):
+        def load_factor(src, name, queue):
             t = new([P, PACK], F32, name)
-            nc.sync.dma_start(t[:], src.rearrange("(p t) o -> p (t o)", t=PACK))
+            queue.dma_start(t[:], src.rearrange("(p t) o -> p (t o)", t=PACK))
             return t
 
         e_plane = new([P, T], U8, "e_plane")
         x_plane = new([P, T], U8, "x_plane")
         w2_plane = new([P, H], U8, "w2_plane")
         w1_plane = new([P, H], U8, "w1_plane")
-        for plane in (e_plane, w2_plane, x_plane, w1_plane):
+        nc.vector.memset(e_plane[:, : T // 2].bitcast(I32), 0)
+        nc.gpsimd.memset(e_plane[:, T // 2 :].bitcast(I32), 0)
+        nc.gpsimd.memset(x_plane[:].bitcast(I32), 0)
+        for plane in (w2_plane, w1_plane):
             nc.vector.memset(plane[:].bitcast(I32), 0)
+        load_scales(x_plane, x_scales, nc.gpsimd)
 
         tgt_sb = load_list(tgt, "tgt_sb")
-        load_scales(e_plane, e_scales)
+        load_scales(e_plane, e_scales, nc.sync)
+        w2_raw = load_weight_words(w2_words, "w2_raw", nc.sync)
+        unit2_sb = load_factor(unit2, "unit2_sb", nc.sync)
         e_table = load_table(e_words, "e_table")
-        w2_raw = load_weight_words(w2_words, "w2_raw")
-        load_scales(w2_plane, w2_scales)
-        unit2_sb = load_factor(unit2, "unit2_sb")
-        x_table = load_table(x_words, "x_table")
+        load_scales(w2_plane, w2_scales, nc.sync)
         offs_sb = load_list(offs, "offs_sb")
-        load_scales(x_plane, x_scales)
+        x_table = load_table(x_words, "x_table")
+        w1_raw = load_weight_words(w1_words, "w1_raw", nc.sync)
+        load_scales(w1_plane, w1_scales, nc.sync)
+        unit_sb = load_factor(unit, "unit_sb", nc.sync)
         mor_sb = load_list(mor, "mor_sb")
-        w1_raw = load_weight_words(w1_words, "w1_raw")
-        load_scales(w1_plane, w1_scales)
-        unit_sb = load_factor(unit, "unit_sb")
         dia_sb = load_list(dia, "dia_sb")
         fert_sb = new([P, T], F32, "fert_sb")
         nc.sync.dma_start(fert_sb[:], fert)
@@ -166,25 +170,26 @@ def tile_picked_ywordal_geo_p_kernel(
         hid_codes = new([P, V], U32, "hid_codes")
         hid_scales = new([P, V], U8, "hid_scales")
 
-        related = new([P, PACK, S], F32, "related")
+        related0 = new([P, PACK, 128], F32, "related0")
+        related = [related0[:], first[:], small[:, 0:2, :].rearrange("p a (b e) -> p (a b) e", b=2)]
         hid2 = new([P, S, PACK], BF16, "hid2")
         hid2_codes = new([P, S], U32, "hid2_codes")
         hid2_scales = new([P, S], U8, "hid2_scales")
-        for h in range(2):
-            cols = slice(HALF * h, HALF * (h + 1))
+        for (lo, hi), rel in zip(PIECES, related):
+            cols = slice(lo, hi)
             for t in range(PACK):
                 nc.scalar.activation(
-                    related[:, t, cols],
-                    ye_sb[:, t, :].indirect(mor_sb[:, 16 * h : 16 * (h + 1)]),
+                    rel[:, t, :],
+                    ye_sb[:, t, :].indirect(mor_sb[:, lo // 16 : hi // 16]),
                     ACT.Copy, scale=0.7,
                 )
             nc.vector.tensor_tensor(
                 hid2[:, cols, :].rearrange("p (c i) t -> p c t i", i=4),
-                related[:, :, cols].rearrange("p t (c i) -> p c t i", i=4),
+                rel.rearrange("p t (c i) -> p c t i", i=4),
                 ye_sb[:, :, cols].rearrange("p t (c i) -> p c t i", i=4),
                 ALU.max,
             )
-            if h == 0:
+            if lo == PIECES[1][0]:
                 nc.vector.quantize_mx(
                     out=hid_codes[:].bitcast(FP8X4), scales=hid_scales[:],
                     in_=hid[:].rearrange("p v t -> p (v t)"),
@@ -194,12 +199,12 @@ def tile_picked_ywordal_geo_p_kernel(
                 in_=hid2[:, cols, :].rearrange("p e t -> p (e t)"),
             )
 
-        fert_pick = new([P, S], F32, "fert_pick")
-        nc.scalar.activation(fert_pick[:], fert_sb[:].indirect(tgt_sb[:]), ACT.Copy, scale=0.2)
+        fert_pick = big[:, 0:2, :].rearrange("p a v -> p (a v)")
+        nc.scalar.activation(fert_pick, fert_sb[:].indirect(tgt_sb[:]), ACT.Copy, scale=0.2)
 
         sc = [ps.tile([P, S], F32, name="ye%d" % m) for m in range(2)]
-        for h in range(2):
-            cols = slice(HALF * h, HALF * (h + 1))
+        for lo, hi in PIECES:
+            cols = slice(lo, hi)
             for m in range(2):
                 rows = slice(P * m, P * (m + 1))
                 nc.tensor.matmul_mx(
@@ -223,7 +228,10 @@ def tile_picked_ywordal_geo_p_kernel(
         inv = new([P, 2], F32, "inv")
         gain = new([P, 2], F32, "gain")
         for m in range(2):
-            nc.vector.tensor_copy(ew_copy[m][:], ew[m][:])
+            if m == 0:
+                nc.vector.tensor_copy(ew_copy[m][:], ew[m][:])
+            else:
+                nc.scalar.copy(ew_copy[m][:], ew[m][:])
             for h in range(2):
                 cols = slice(HALF * h, HALF * (h + 1))
                 nc.vector.tensor_tensor(
@@ -234,7 +242,8 @@ def tile_picked_ywordal_geo_p_kernel(
                 nc.vector.reciprocal(inv[:], tot[:])
                 nc.vector.scalar_tensor_tensor(gain[:], inv[:], 2500.0, inv[:], ALU.mult, ALU.mult)
         for m in range(2):
-            nc.vector.tensor_tensor(side[m][:], sc[m][:], fert_pick[:], ALU.mult)
-            nc.scalar.activation(root[m][:], prod[m][:], ACT.Sqrt, bias=0.01, scale=gain[:, m : m + 1])
-            nc.vector.tensor_tensor(res[m][:], root[m][:], side[m][:], ALU.add)
-            nc.sync.dma_start(out[P * m : P * (m + 1), :], res[m][:])
+            nc.vector.tensor_tensor(side[m][:], sc[m][:], fert_pick, ALU.mult)
+        for m, lo, hi in ((0, 0, S), (1, 0, HALF), (1, HALF, S)):
+            nc.scalar.activation(root[m][:, lo:hi], prod[m][:, lo:hi], ACT.Sqrt, bias=0.01, scale=gain[:, m : m + 1])
+            nc.vector.tensor_tensor(res[m][:, lo:hi], root[m][:, lo:hi], side[m][:, lo:hi], ALU.add)
+            nc.sync.dma_start(out[P * m : P * (m + 1), lo:hi], res[m][:, lo:hi])

@@ -15,7 +15,6 @@ FP8X4 = mybir.dt.float8_e4m3fn_x4
 FP4X4 = mybir.dt.float4_e2m1fn_x4
 ALU = mybir.AluOpType
 ACT = mybir.ActivationFunctionType
-AX = mybir.AxisListType
 
 P = 128
 PACK = 4
@@ -32,8 +31,8 @@ def tile_picked_ywordal_geo_p_kernel(
         sb = ctx.enter_context(tc.tile_pool(name="sb", bufs=1))
         ps = ctx.enter_context(tc.psum_pool(name="ps", bufs=1))
 
-        def new(shape, dtype, name):
-            return sb.tile(shape, dtype, name=name, align_bytes=64)
+        def new(shape, dtype, name, tag=None):
+            return sb.tile(shape, dtype, name=name, tag=tag or name, align_bytes=64)
 
         def load_list(src, name):
             t = sb.tile([P, S // 16], U16, name=name)
@@ -57,125 +56,146 @@ def tile_picked_ywordal_geo_p_kernel(
             queue.dma_start(t[:].bitcast(I32), src[0].bitcast(I32))
             return t
 
-        def load_factor(src, name, queue):
+        def load_factor(src, name):
             t = new([P, PACK], F32, name)
-            queue.dma_start(t[:], src.rearrange("(p t) o -> p (t o)", t=PACK))
+            nc.sync.dma_start(t[:], src.rearrange("(p t) o -> p (t o)", t=PACK))
             return t
 
         e_plane = new([P, T], U8, "e_plane")
         x_plane = new([P, T], U8, "x_plane")
+        w2_landing = new([P, H], U8, "w2_landing")
         w2_plane = new([P, H], U8, "w2_plane")
         w1_plane = new([P, H], U8, "w1_plane")
-        nc.vector.memset(e_plane[:, : T // 2].bitcast(I32), 0)
-        nc.gpsimd.memset(e_plane[:, T // 2 :].bitcast(I32), 0)
-        nc.gpsimd.memset(x_plane[:].bitcast(I32), 0)
-        for plane in (w2_plane, w1_plane):
+        for plane in (e_plane, w2_plane, x_plane):
             nc.vector.memset(plane[:].bitcast(I32), 0)
-        load_scales(x_plane, x_scales, nc.gpsimd)
+        nc.gpsimd.memset(w1_plane[:].bitcast(I32), 0)
+        w1_raw = load_weight_words(w1_words, "w1_raw", nc.gpsimd)
+        load_scales(w1_plane, w1_scales, nc.gpsimd)
 
+        unit2_sb = load_factor(unit2, "unit2_sb")
+        unit_sb = load_factor(unit, "unit_sb")
         tgt_sb = load_list(tgt, "tgt_sb")
-        load_scales(e_plane, e_scales, nc.sync)
-        w2_raw = load_weight_words(w2_words, "w2_raw", nc.sync)
-        unit2_sb = load_factor(unit2, "unit2_sb", nc.sync)
+        load_scales(w2_landing, w2_scales, nc.sync)
         e_table = load_table(e_words, "e_table")
-        load_scales(w2_plane, w2_scales, nc.sync)
-        offs_sb = load_list(offs, "offs_sb")
-        x_table = load_table(x_words, "x_table")
-        w1_raw = load_weight_words(w1_words, "w1_raw", nc.sync)
-        load_scales(w1_plane, w1_scales, nc.sync)
-        unit_sb = load_factor(unit, "unit_sb", nc.sync)
         mor_sb = load_list(mor, "mor_sb")
+        w2_raw = load_weight_words(w2_words, "w2_raw", nc.sync)
+        load_scales(e_plane, e_scales, nc.sync)
+        x_table = load_table(x_words, "x_table")
+        offs_sb = load_list(offs, "offs_sb")
+        load_scales(x_plane, x_scales, nc.sync)
         dia_sb = load_list(dia, "dia_sb")
-        fert_sb = new([P, T], F32, "fert_sb")
-        nc.sync.dma_start(fert_sb[:], fert)
 
-        def deal(raw, plane, name):
-            words = new([P, 2 * H], U8, name + "_words")
-            scales = new([P, H], U8, name + "_scales")
+        def deal_words(raw, name):
+            words = new([P, 2 * H], U8, name)
             nc.scalar.copy(
                 words[:].bitcast(U16).rearrange("p (t m) -> p t m", t=PACK),
                 raw[:].bitcast(U16).rearrange("p (m t) -> p t m", t=PACK),
             )
-            nc.gpsimd.tensor_copy(
+            return words
+
+        def deal_scales(plane, engine, name):
+            scales = new([P, H], U8, name)
+            engine.tensor_copy(
                 scales[:].rearrange("p (t m) -> p t m", t=PACK),
                 plane[:].rearrange("p (m t) -> p t m", t=PACK),
             )
-            return words, scales
+            return scales
 
         def pick(table, plane, lst, name):
             scales = new([P, S], U8, name + "_scales")
             words = new([P, S], U32, name + "_words")
-            nc.vector.tensor_copy(scales[:], plane[:].indirect(lst[:]))
-            nc.vector.tensor_copy(words[:], table[:].bitcast(U32).indirect(lst[:]))
+            for h in range(2):
+                cols = slice(HALF * h, HALF * (h + 1))
+                part = lst[:, 16 * h : 16 * (h + 1)]
+                nc.vector.tensor_copy(words[:, cols], table[:].bitcast(U32).indirect(part))
+                nc.vector.tensor_copy(scales[:, cols], plane[:].indirect(part))
             return words, scales
 
-        def first_product(w, picked, tag):
-            banks = []
+        def first_product(w_words, w_scales, picked, tag):
+            banks = [ps.tile([P, S], F32, name="%s%d" % (tag, t)) for t in range(PACK)]
             for t in range(PACK):
-                bank = ps.tile([P, S], F32, name="%s%d" % (tag, t))
-                nc.tensor.matmul_mx(
-                    out=bank[:],
-                    lhsT=w[0][:, 2 * P * t : 2 * P * (t + 1)].bitcast(FP4X4),
-                    lhsT_scale=w[1][:, P * t : P * (t + 1)],
-                    rhs=picked[0][:].bitcast(FP8X4),
-                    rhs_scale=picked[1][:],
-                    start=True, stop=True,
-                )
-                banks.append(bank)
+                for h in range(2):
+                    cols = slice(HALF * h, HALF * (h + 1))
+                    nc.tensor.matmul_mx(
+                        out=banks[t][:, cols],
+                        lhsT=w_words[:, 2 * P * t : 2 * P * (t + 1)].bitcast(FP4X4),
+                        lhsT_scale=w_scales[:, P * t : P * (t + 1)],
+                        rhs=picked[0][:, cols].bitcast(FP8X4),
+                        rhs_scale=picked[1][:, cols],
+                        start=True, stop=True,
+                    )
             return banks
 
-        size2 = new([P, PACK], F32, "size2")
-        sign2 = new([P, PACK], F32, "sign2")
-        nc.scalar.activation(size2[:], unit2_sb[:], ACT.Abs)
-        nc.scalar.activation(sign2[:], unit2_sb[:], ACT.Sign)
-        w2 = deal(w2_raw, w2_plane, "w2")
-        e_pick = pick(e_table, e_plane, tgt_sb, "e_pick")
-        ye = first_product(w2, e_pick, "ye")
-        ye_sb = new([P, PACK, S], F32, "ye_sb")
-        for t in range(PACK):
-            nc.scalar.activation(ye_sb[:, t, :], ye[t][:], ACT.Copy, scale=size2[:, t : t + 1])
-
-        x_pick = pick(x_table, x_plane, offs_sb, "x_pick")
-        w1 = deal(w1_raw, w1_plane, "w1")
-        y = first_product(w1, x_pick, "y")
+        size2 = new([P, PACK - 1], F32, "size2")
+        twice_pos2 = new([P, PACK], F32, "twice_pos2")
         fac = new([P, PACK], F32, "fac")
-        pos = new([P, PACK], F32, "pos")
-        beta = new([P, PACK], F32, "beta")
-        rho = new([P, PACK], F32, "rho")
+        fac_hi = new([P, PACK], F32, "fac_hi")
         fac_lo = new([P, PACK], F32, "fac_lo")
-        nc.gpsimd.tensor_tensor(fac[:], unit_sb[:], sign2[:], ALU.mult)
-        nc.gpsimd.tensor_scalar(pos[:], fac[:], 0.0, None, ALU.is_ge)
-        nc.gpsimd.tensor_scalar(beta[:], pos[:], -0.5, 1.0, ALU.mult, ALU.add)
-        nc.gpsimd.tensor_scalar(rho[:], pos[:], 1.5, 0.5, ALU.mult, ALU.add)
-        nc.gpsimd.tensor_tensor(fac_lo[:], fac[:], beta[:], ALU.mult)
+        nc.scalar.activation(size2[:], unit2_sb[:, : PACK - 1], ACT.Abs)
+        nc.vector.tensor_scalar(twice_pos2[:], unit2_sb[:], 0.0, 2.0, ALU.is_ge, ALU.mult)
+        nc.vector.scalar_tensor_tensor(fac[:], twice_pos2[:], -1.0, unit_sb[:], ALU.add, ALU.mult)
+        nc.vector.scalar_tensor_tensor(fac_hi[:], fac[:], 0.5, fac[:], ALU.mult, ALU.max)
+        nc.vector.scalar_tensor_tensor(fac_lo[:], fac[:], 0.5, fac[:], ALU.mult, ALU.min)
 
-        first = new([P, PACK, V], F32, "first")
+        ratio_less2 = new([P, PACK], F32, "ratio_less2")
+        ratio = new([P, PACK], F32, "ratio")
+        nc.vector.tensor_scalar(ratio_less2[:], fac[:], 0.0, -1.5, ALU.is_ge, ALU.mult)
+        nc.vector.tensor_scalar(ratio[:], ratio_less2[:], 2.0, None, ALU.add)
+
+        for q in range(4):
+            rows = slice(32 * q, 32 * q + 4)
+            nc.vector.tensor_copy(w2_plane[rows, :].bitcast(I32), w2_landing[rows, :].bitcast(I32))
+        w2_dealt = deal_scales(w2_plane, nc.vector, "w2_dealt")
+        w1_dealt = deal_scales(w1_plane, nc.gpsimd, "w1_dealt")
+        w2_codes = deal_words(w2_raw, "w2_codes")
+        w1_codes = deal_words(w1_raw, "w1_codes")
+        e_pick = pick(e_table, e_plane, tgt_sb, "e_pick")
+        ye = first_product(w2_codes, w2_dealt, e_pick, "ye")
+        x_pick = pick(x_table, x_plane, offs_sb, "x_pick")
+        y = first_product(w1_codes, w1_dealt, x_pick, "y")
+        ye_sb = new([P, PACK, S], F32, "ye_sb")
+        for t in range(PACK - 1):
+            nc.scalar.activation(ye_sb[:, t, :], ye[t][:], ACT.Copy, scale=size2[:, t : t + 1])
+        size2_last = new([P, 1], F32, "size2_last", tag="x_plane")
+        last = slice(PACK - 1, PACK)
+        nc.vector.scalar_tensor_tensor(size2_last[:], unit2_sb[:, last], -1.0, unit2_sb[:, last], ALU.mult, ALU.max)
+        nc.vector.tensor_scalar(ye_sb[:, PACK - 1, :], ye[PACK - 1][:], size2_last[:], None, ALU.mult)
+
+        fert_sb = new([P, T], F32, "fert_sb", tag="size2")
+        nc.sync.dma_start(fert_sb[:], fert)
+
+        first_hi = new([P, PACK, V], F32, "first_hi")
+        first_lo = new([P, PACK, V], F32, "first_lo")
         big = new([P, PACK, V], F32, "big")
         small = new([P, PACK, V], F32, "small")
-        hid_rows = new([P, PACK, V], BF16, "hid_rows")
         for t in range(PACK):
             pair = y[t][:].rearrange("p (v d) -> p v d", d=2)
-            col = fac_lo[:, t : t + 1]
-            nc.scalar.activation(first[:, t, :], pair[:, :, 0], ACT.Copy, scale=col)
-            nc.vector.scalar_tensor_tensor(big[:, t, :], pair[:, :, 1], col, first[:, t, :], ALU.mult, ALU.max)
-            nc.vector.scalar_tensor_tensor(small[:, t, :], pair[:, :, 1], col, first[:, t, :], ALU.mult, ALU.min)
-        for t in range(PACK):
+            row = slice(t, t + 1)
+            nc.scalar.activation(first_hi[:, t, :], pair[:, :, 0], ACT.Copy, scale=fac_hi[:, row])
+            nc.gpsimd.tensor_scalar(first_lo[:, t, :], first_hi[:, t, :], ratio[:, row], 0.0, ALU.mult, ALU.add)
             nc.vector.scalar_tensor_tensor(
-                hid_rows[:, t, :], big[:, t, :], rho[:, t : t + 1], small[:, t, :], ALU.mult, ALU.add)
+                big[:, t, :], pair[:, :, 1], fac_hi[:, row], first_hi[:, t, :], ALU.mult, ALU.max)
+            nc.vector.scalar_tensor_tensor(
+                small[:, t, :], pair[:, :, 1], fac_lo[:, row], first_lo[:, t, :], ALU.mult, ALU.min)
         hid = new([P, V, PACK], BF16, "hid")
-        nc.vector.tensor_copy(
+        nc.vector.tensor_tensor(
             hid[:].rearrange("p (c i) t -> p c t i", i=4),
-            hid_rows[:].rearrange("p t (c i) -> p c t i", i=4),
+            big[:].rearrange("p t (c i) -> p c t i", i=4),
+            small[:].rearrange("p t (c i) -> p c t i", i=4),
+            ALU.add,
         )
         hid_codes = new([P, V], U32, "hid_codes")
         hid_scales = new([P, V], U8, "hid_scales")
 
         related0 = new([P, PACK, 128], F32, "related0")
-        related = [related0[:], first[:], small[:, 0:2, :].rearrange("p a (b e) -> p (a b) e", b=2)]
-        hid2 = new([P, S, PACK], BF16, "hid2")
+        related = [
+            related0[:],
+            first_lo[:],
+            first_hi[:, 0:2, :].rearrange("p a (b e) -> p (a b) e", b=2),
+        ]
         hid2_codes = new([P, S], U32, "hid2_codes")
         hid2_scales = new([P, S], U8, "hid2_scales")
-        for (lo, hi), rel in zip(PIECES, related):
+        for (lo, hi), rel, tag in zip(PIECES, related, ("x_plane", "hid", "x_plane")):
             cols = slice(lo, hi)
             for t in range(PACK):
                 nc.scalar.activation(
@@ -183,66 +203,74 @@ def tile_picked_ywordal_geo_p_kernel(
                     ye_sb[:, t, :].indirect(mor_sb[:, lo // 16 : hi // 16]),
                     ACT.Copy, scale=0.7,
                 )
+            hid2 = new([P, hi - lo, PACK], BF16, "hid2_%d" % lo, tag=tag)
             nc.vector.tensor_tensor(
-                hid2[:, cols, :].rearrange("p (c i) t -> p c t i", i=4),
+                hid2[:].rearrange("p (c i) t -> p c t i", i=4),
                 rel.rearrange("p t (c i) -> p c t i", i=4),
                 ye_sb[:, :, cols].rearrange("p t (c i) -> p c t i", i=4),
                 ALU.max,
             )
-            if lo == PIECES[1][0]:
+            if lo == 0:
                 nc.vector.quantize_mx(
                     out=hid_codes[:].bitcast(FP8X4), scales=hid_scales[:],
                     in_=hid[:].rearrange("p v t -> p (v t)"),
                 )
             nc.vector.quantize_mx(
                 out=hid2_codes[:, cols].bitcast(FP8X4), scales=hid2_scales[:, cols],
-                in_=hid2[:, cols, :].rearrange("p e t -> p (e t)"),
+                in_=hid2[:].rearrange("p e t -> p (e t)"),
             )
 
         fert_pick = big[:, 0:2, :].rearrange("p a v -> p (a v)")
-        nc.scalar.activation(fert_pick, fert_sb[:].indirect(tgt_sb[:]), ACT.Copy, scale=0.2)
+        nc.scalar.activation(fert_pick, fert_sb[:].indirect(tgt_sb[:]), ACT.Copy, scale=-0.2)
 
-        sc = [ps.tile([P, S], F32, name="ye%d" % m) for m in range(2)]
+        early = [ps.tile([P, S], F32, name="ye%d" % m) for m in range(2)]
+        late = [ps.tile([P, S], F32, name="ye%d" % (2 + m)) for m in range(2)]
+        cut = PIECES[-1][0]
         for lo, hi in PIECES:
             cols = slice(lo, hi)
             for m in range(2):
                 rows = slice(P * m, P * (m + 1))
                 nc.tensor.matmul_mx(
-                    out=sc[m][:, cols],
+                    out=(early if lo < cut else late)[m][:, cols],
                     lhsT=hid_codes[:, rows].bitcast(FP8X4), lhsT_scale=hid_scales[:, rows],
                     rhs=hid2_codes[:, cols].bitcast(FP8X4), rhs_scale=hid2_scales[:, cols],
                     start=True, stop=True,
                 )
 
-        neg_top = [new([P, 1], F32, "neg_top%d" % m) for m in range(2)]
+        neg_top = [new([P, 2], F32, "neg_top%d" % m) for m in range(2)]
+        neg_both = new([P, 2, S], F32, "neg_both", tag="x_plane")
+        neg = [neg_both[:, m, :] for m in range(2)]
         tot = new([P, 2], F32, "tot")
         ew = [new([P, S], F32, "ew%d" % m) for m in range(2)]
-        ew_copy = [new([P, S], F32, "ew_copy%d" % m) for m in range(2)]
+        ew_dia = [new([P, S], F32, "ew_dia%d" % m) for m in range(2)]
         prod = [new([P, S], F32, "prod%d" % m) for m in range(2)]
         side = [new([P, S], F32, "side%d" % m) for m in range(2)]
         root = [new([P, S], F32, "root%d" % m) for m in range(2)]
         res = [new([P, S], F32, "res%d" % m) for m in range(2)]
         for m in range(2):
-            nc.vector.tensor_reduce(neg_top[m][:], sc[m][:], AX.X, ALU.max, negate=True)
-            nc.scalar.activation(ew[m][:], sc[m][:], ACT.Exp, bias=neg_top[m][:], accum_out=tot[:, m : m + 1])
+            nc.vector.tensor_scalar(
+                neg[m][:, :cut], early[m][:, :cut], -1.0, None, ALU.mult, ALU.min, accum_out=neg_top[m][:, 0:1])
+            nc.vector.tensor_scalar(
+                neg[m][:, cut:], late[m][:, cut:], -1.0, neg_top[m][:, 0:1], ALU.mult, ALU.min,
+                accum_out=neg_top[m][:, 1:2])
+            nc.scalar.activation(
+                ew[m][:], neg[m], ACT.Exp, bias=neg_top[m][:, 1:2], scale=-1.0, accum_out=tot[:, m : m + 1])
         inv = new([P, 2], F32, "inv")
         gain = new([P, 2], F32, "gain")
+        halves = [(slice(HALF * h, HALF * (h + 1)), dia_sb[:, 16 * h : 16 * (h + 1)]) for h in range(2)]
+        for cols, part in halves:
+            nc.vector.tensor_copy(ew_dia[0][:, cols], ew[0][:].indirect(part))
+        nc.vector.tensor_tensor(prod[0][:], ew_dia[0][:], ew[0][:], ALU.mult)
+        nc.vector.reciprocal(inv[:], tot[:])
+        cols, part = halves[0]
+        nc.scalar.activation(ew_dia[1][:, cols], ew[1][:].indirect(part), ACT.Copy)
+        nc.vector.tensor_tensor(prod[1][:, cols], ew_dia[1][:, cols], ew[1][:, cols], ALU.mult)
+        nc.vector.scalar_tensor_tensor(gain[:], inv[:], 2500.0, inv[:], ALU.mult, ALU.mult)
+        cols, part = halves[1]
+        nc.vector.tensor_copy(ew_dia[1][:, cols], ew[1][:].indirect(part))
+        nc.vector.tensor_tensor(prod[1][:, cols], ew_dia[1][:, cols], ew[1][:, cols], ALU.mult)
         for m in range(2):
-            if m == 0:
-                nc.vector.tensor_copy(ew_copy[m][:], ew[m][:])
-            else:
-                nc.scalar.copy(ew_copy[m][:], ew[m][:])
-            for h in range(2):
-                cols = slice(HALF * h, HALF * (h + 1))
-                nc.vector.tensor_tensor(
-                    prod[m][:, cols], ew[m][:].indirect(dia_sb[:, 16 * h : 16 * (h + 1)]),
-                    ew_copy[m][:, cols], ALU.mult,
-                )
-            if m == 0:
-                nc.vector.reciprocal(inv[:], tot[:])
-                nc.vector.scalar_tensor_tensor(gain[:], inv[:], 2500.0, inv[:], ALU.mult, ALU.mult)
-        for m in range(2):
-            nc.vector.tensor_tensor(side[m][:], sc[m][:], fert_pick, ALU.mult)
+            nc.vector.tensor_tensor(side[m][:], neg[m], fert_pick, ALU.mult)
         for m, lo, hi in ((0, 0, S), (1, 0, HALF), (1, HALF, S)):
             nc.scalar.activation(root[m][:, lo:hi], prod[m][:, lo:hi], ACT.Sqrt, bias=0.01, scale=gain[:, m : m + 1])
             nc.vector.tensor_tensor(res[m][:, lo:hi], root[m][:, lo:hi], side[m][:, lo:hi], ALU.add)

from contextlib import ExitStack

import concourse.mybir as mybir

K, T, S, H, V = 512, 2048, 512, 512, 256
FLOPS = 2 * K * H * S * 2 + 2 * H * V * S

F32 = mybir.dt.float32
BF16 = mybir.dt.bfloat16
I32 = mybir.dt.int32
U32 = mybir.dt.uint32
U16 = mybir.dt.uint16
U8 = mybir.dt.uint8
FP8X4 = mybir.dt.float8_e4m3fn_x4
FP4X4 = mybir.dt.float4_e2m1fn_x4
ALU = mybir.AluOpType
ACT = mybir.ActivationFunctionType

P = 128
PACK = 4
HALF = S // 2
PIECES = ((0, 128), (128, 384), (384, 512))


def tile_picked_ywordal_geo_p_kernel(
    tc, x_words, x_scales, w1_words, w1_scales, e_words, e_scales, w2_words, w2_scales,
    unit, unit2, fert, offs, tgt, mor, dia, out,
):
    nc = tc.nc
    with ExitStack() as ctx:
        sb = ctx.enter_context(tc.tile_pool(name="sb", bufs=1))
        ps = ctx.enter_context(tc.psum_pool(name="ps", bufs=1))

        def new(shape, dtype, name, tag=None):
            return sb.tile(shape, dtype, name=name, tag=tag or name, align_bytes=64)

        def load_list(src, name):
            t = sb.tile([P, S // 16], U16, name=name)
            nc.sync.dma_start(t[:], src)
            return t

        def load_scales(plane, src, queue):
            for q in range(4):
                queue.dma_start(
                    plane[32 * q : 32 * q + 4, :].bitcast(I32),
                    src[0, 4 * q : 4 * q + 4, :].bitcast(I32),
                )

        def load_table(src, name):
            t = new([P, T], I32, name)
            nc.sync.dma_start(t[:], src[0].rearrange("p n r -> p (n r)").bitcast(I32))
            return t

        def load_weight_words(src, name, queue):
            t = new([P, 2 * H], U8, name)
            queue.dma_start(t[:].bitcast(I32), src[0].bitcast(I32))
            return t

        def load_factor(src, name):
            t = new([P, PACK], F32, name)
            nc.sync.dma_start(t[:], src.rearrange("(p t) o -> p (t o)", t=PACK))
            return t

        e_plane = new([P, T], U8, "e_plane")
        x_plane = new([P, T], U8, "x_plane")
        w2_landing = new([P, H], U8, "w2_landing")
        w2_plane = new([P, H], U8, "w2_plane")
        w1_plane = new([P, H], U8, "w1_plane")
        for plane in (e_plane, w2_plane, x_plane):
            nc.vector.memset(plane[:].bitcast(I32), 0)
        nc.gpsimd.memset(w1_plane[:].bitcast(I32), 0)
        w1_raw = load_weight_words(w1_words, "w1_raw", nc.gpsimd)
        load_scales(w1_plane, w1_scales, nc.gpsimd)

        unit2_sb = load_factor(unit2, "unit2_sb")
        unit_sb = load_factor(unit, "unit_sb")
        tgt_sb = load_list(tgt, "tgt_sb")
        load_scales(w2_landing, w2_scales, nc.sync)
        e_table = load_table(e_words, "e_table")
        mor_sb = load_list(mor, "mor_sb")
        w2_raw = load_weight_words(w2_words, "w2_raw", nc.sync)
        load_scales(e_plane, e_scales, nc.sync)
        x_table = load_table(x_words, "x_table")
        offs_sb = load_list(offs, "offs_sb")
        load_scales(x_plane, x_scales, nc.sync)
        dia_sb = load_list(dia, "dia_sb")

        def deal_words(raw, name):
            words = new([P, 2 * H], U8, name)
            nc.scalar.copy(
                words[:].bitcast(U16).rearrange("p (t m) -> p t m", t=PACK),
                raw[:].bitcast(U16).rearrange("p (m t) -> p t m", t=PACK),
            )
            return words

        def deal_scales(plane, engine, name):
            scales = new([P, H], U8, name)
            engine.tensor_copy(
                scales[:].rearrange("p (t m) -> p t m", t=PACK),
                plane[:].rearrange("p (m t) -> p t m", t=PACK),
            )
            return scales

        def pick(table, plane, lst, name):
            scales = new([P, S], U8, name + "_scales")
            words = new([P, S], U32, name + "_words")
            for h in range(2):
                cols = slice(HALF * h, HALF * (h + 1))
                part = lst[:, 16 * h : 16 * (h + 1)]
                nc.vector.tensor_copy(words[:, cols], table[:].bitcast(U32).indirect(part))
                nc.vector.tensor_copy(scales[:, cols], plane[:].indirect(part))
            return words, scales

        def first_product(w_words, w_scales, picked, tag):
            banks = [ps.tile([P, S], F32, name="%s%d" % (tag, t)) for t in range(PACK)]
            for t in range(PACK):
                for h in range(2):
                    cols = slice(HALF * h, HALF * (h + 1))
                    nc.tensor.matmul_mx(
                        out=banks[t][:, cols],
                        lhsT=w_words[:, 2 * P * t : 2 * P * (t + 1)].bitcast(FP4X4),
                        lhsT_scale=w_scales[:, P * t : P * (t + 1)],
                        rhs=picked[0][:, cols].bitcast(FP8X4),
                        rhs_scale=picked[1][:, cols],
                        start=True, stop=True,
                    )
            return banks

        size2 = new([P, PACK - 1], F32, "size2")
        twice_pos2 = new([P, PACK], F32, "twice_pos2")
        fac = new([P, PACK], F32, "fac")
        fac_hi = new([P, PACK], F32, "fac_hi")
        fac_lo = new([P, PACK], F32, "fac_lo")
        nc.scalar.activation(size2[:], unit2_sb[:, : PACK - 1], ACT.Abs)
        nc.vector.tensor_scalar(twice_pos2[:], unit2_sb[:], 0.0, 2.0, ALU.is_ge, ALU.mult)
        nc.vector.scalar_tensor_tensor(fac[:], twice_pos2[:], -1.0, unit_sb[:], ALU.add, ALU.mult)
        nc.vector.scalar_tensor_tensor(fac_hi[:], fac[:], 0.5, fac[:], ALU.mult, ALU.max)
        nc.vector.scalar_tensor_tensor(fac_lo[:], fac[:], 0.5, fac[:], ALU.mult, ALU.min)

        ratio_less2 = new([P, PACK], F32, "ratio_less2")
        ratio = new([P, PACK], F32, "ratio")
        nc.vector.tensor_scalar(ratio_less2[:], fac[:], 0.0, -1.5, ALU.is_ge, ALU.mult)
        nc.vector.tensor_scalar(ratio[:], ratio_less2[:], 2.0, None, ALU.add)

        for q in range(4):
            rows = slice(32 * q, 32 * q + 4)
            nc.vector.tensor_copy(w2_plane[rows, :].bitcast(I32), w2_landing[rows, :].bitcast(I32))
        w2_dealt = deal_scales(w2_plane, nc.vector, "w2_dealt")
        w1_dealt = deal_scales(w1_plane, nc.gpsimd, "w1_dealt")
        w2_codes = deal_words(w2_raw, "w2_codes")
        w1_codes = deal_words(w1_raw, "w1_codes")
        e_pick = pick(e_table, e_plane, tgt_sb, "e_pick")
        ye = first_product(w2_codes, w2_dealt, e_pick, "ye")
        x_pick = pick(x_table, x_plane, offs_sb, "x_pick")
        y = first_product(w1_codes, w1_dealt, x_pick, "y")
        ye_sb = new([P, PACK, S], F32, "ye_sb")
        for t in range(PACK - 1):
            nc.scalar.activation(ye_sb[:, t, :], ye[t][:], ACT.Copy, scale=size2[:, t : t + 1])
        size2_last = new([P, 1], F32, "size2_last", tag="x_plane")
        last = slice(PACK - 1, PACK)
        nc.vector.scalar_tensor_tensor(size2_last[:], unit2_sb[:, last], -1.0, unit2_sb[:, last], ALU.mult, ALU.max)
        nc.vector.tensor_scalar(ye_sb[:, PACK - 1, :], ye[PACK - 1][:], size2_last[:], None, ALU.mult)

        fert_sb = new([P, T], F32, "fert_sb", tag="size2")
        nc.sync.dma_start(fert_sb[:], fert)

        first_hi = new([P, PACK, V], F32, "first_hi")
        first_lo = new([P, PACK, V], F32, "first_lo")
        big = new([P, PACK, V], F32, "big")
        small = new([P, PACK, V], F32, "small")
        for t in range(PACK):
            pair = y[t][:].rearrange("p (v d) -> p v d", d=2)
            row = slice(t, t + 1)
            nc.scalar.activation(first_hi[:, t, :], pair[:, :, 0], ACT.Copy, scale=fac_hi[:, row])
            nc.gpsimd.tensor_scalar(first_lo[:, t, :], first_hi[:, t, :], ratio[:, row], 0.0, ALU.mult, ALU.add)
            nc.vector.scalar_tensor_tensor(
                big[:, t, :], pair[:, :, 1], fac_hi[:, row], first_hi[:, t, :], ALU.mult, ALU.max)
            nc.vector.scalar_tensor_tensor(
                small[:, t, :], pair[:, :, 1], fac_lo[:, row], first_lo[:, t, :], ALU.mult, ALU.min)
        hid = new([P, V, PACK], BF16, "hid")
        nc.vector.tensor_tensor(
            hid[:].rearrange("p (c i) t -> p c t i", i=4),
            big[:].rearrange("p t (c i) -> p c t i", i=4),
            small[:].rearrange("p t (c i) -> p c t i", i=4),
            ALU.add,
        )
        hid_codes = new([P, V], U32, "hid_codes")
        hid_scales = new([P, V], U8, "hid_scales")

        related0 = new([P, PACK, 128], F32, "related0")
        related = [
            related0[:],
            first_lo[:],
            first_hi[:, 0:2, :].rearrange("p a (b e) -> p (a b) e", b=2),
        ]
        hid2_codes = new([P, S], U32, "hid2_codes")
        hid2_scales = new([P, S], U8, "hid2_scales")
        for (lo, hi), rel, tag in zip(PIECES, related, ("x_plane", "hid", "x_plane")):
            cols = slice(lo, hi)
            for t in range(PACK):
                nc.scalar.activation(
                    rel[:, t, :],
                    ye_sb[:, t, :].indirect(mor_sb[:, lo // 16 : hi // 16]),
                    ACT.Copy, scale=0.7,
                )
            hid2 = new([P, hi - lo, PACK], BF16, "hid2_%d" % lo, tag=tag)
            nc.vector.tensor_tensor(
                hid2[:].rearrange("p (c i) t -> p c t i", i=4),
                rel.rearrange("p t (c i) -> p c t i", i=4),
                ye_sb[:, :, cols].rearrange("p t (c i) -> p c t i", i=4),
                ALU.max,
            )
            if lo == 0:
                nc.vector.quantize_mx(
                    out=hid_codes[:].bitcast(FP8X4), scales=hid_scales[:],
                    in_=hid[:].rearrange("p v t -> p (v t)"),
                )
            nc.vector.quantize_mx(
                out=hid2_codes[:, cols].bitcast(FP8X4), scales=hid2_scales[:, cols],
                in_=hid2[:].rearrange("p e t -> p (e t)"),
            )

        fert_pick = big[:, 0:2, :].rearrange("p a v -> p (a v)")
        nc.scalar.activation(fert_pick, fert_sb[:].indirect(tgt_sb[:]), ACT.Copy, scale=-0.2)

        early = [ps.tile([P, S], F32, name="ye%d" % m) for m in range(2)]
        late = [ps.tile([P, S], F32, name="ye%d" % (2 + m)) for m in range(2)]
        cut = PIECES[-1][0]
        for lo, hi in PIECES:
            cols = slice(lo, hi)
            for m in range(2):
                rows = slice(P * m, P * (m + 1))
                nc.tensor.matmul_mx(
                    out=(early if lo < cut else late)[m][:, cols],
                    lhsT=hid_codes[:, rows].bitcast(FP8X4), lhsT_scale=hid_scales[:, rows],
                    rhs=hid2_codes[:, cols].bitcast(FP8X4), rhs_scale=hid2_scales[:, cols],
                    start=True, stop=True,
                )

        neg_top = [new([P, 2], F32, "neg_top%d" % m) for m in range(2)]
        neg_both = new([P, 2, S], F32, "neg_both", tag="x_plane")
        neg = [neg_both[:, m, :] for m in range(2)]
        tot = new([P, 2], F32, "tot")
        ew = [new([P, S], F32, "ew%d" % m) for m in range(2)]
        ew_dia = [new([P, S], F32, "ew_dia%d" % m) for m in range(2)]
        prod = [new([P, S], F32, "prod%d" % m) for m in range(2)]
        side = [new([P, S], F32, "side%d" % m) for m in range(2)]
        root = [new([P, S], F32, "root%d" % m) for m in range(2)]
        res = [new([P, S], F32, "res%d" % m) for m in range(2)]
        for m in range(2):
            nc.vector.tensor_scalar(
                neg[m][:, :cut], early[m][:, :cut], -1.0, None, ALU.mult, ALU.min, accum_out=neg_top[m][:, 0:1])
            nc.vector.tensor_scalar(
                neg[m][:, cut:], late[m][:, cut:], -1.0, neg_top[m][:, 0:1], ALU.mult, ALU.min,
                accum_out=neg_top[m][:, 1:2])
            nc.scalar.activation(
                ew[m][:], neg[m], ACT.Exp, bias=neg_top[m][:, 1:2], scale=-1.0, accum_out=tot[:, m : m + 1])
        inv = new([P, 2], F32, "inv")
        gain = new([P, 2], F32, "gain")
        halves = [(slice(HALF * h, HALF * (h + 1)), dia_sb[:, 16 * h : 16 * (h + 1)]) for h in range(2)]
        for cols, part in halves:
            nc.vector.tensor_copy(ew_dia[0][:, cols], ew[0][:].indirect(part))
        nc.vector.tensor_tensor(prod[0][:], ew_dia[0][:], ew[0][:], ALU.mult)
        nc.vector.reciprocal(inv[:], tot[:])
        cols, part = halves[0]
        nc.scalar.activation(ew_dia[1][:, cols], ew[1][:].indirect(part), ACT.Copy)
        nc.vector.tensor_tensor(prod[1][:, cols], ew_dia[1][:, cols], ew[1][:, cols], ALU.mult)
        nc.vector.scalar_tensor_tensor(gain[:], inv[:], 2500.0, inv[:], ALU.mult, ALU.mult)
        cols, part = halves[1]
        nc.vector.tensor_copy(ew_dia[1][:, cols], ew[1][:].indirect(part))
        nc.vector.tensor_tensor(prod[1][:, cols], ew_dia[1][:, cols], ew[1][:, cols], ALU.mult)
        for m in range(2):
            nc.vector.tensor_tensor(side[m][:], neg[m], fert_pick, ALU.mult)
        for m, lo, hi in ((0, 0, S), (1, 0, HALF), (1, HALF, S)):
            nc.scalar.activation(root[m][:, lo:hi], prod[m][:, lo:hi], ACT.Sqrt, bias=0.01, scale=gain[:, m : m + 1])
            nc.vector.tensor_tensor(res[m][:, lo:hi], root[m][:, lo:hi], side[m][:, lo:hi], ALU.add)
            nc.sync.dma_start(out[P * m : P * (m + 1), lo:hi], res[m][:, lo:hi])
